import numpy as np
import ml_dtypes


def mxq(x, axis, fmt="e4m3"):
    dtype, down = {"e4m3": (ml_dtypes.float8_e4m3fn, 7), "e5m2": (ml_dtypes.float8_e5m2, 14)}[fmt]
    v = np.moveaxis(np.asarray(x, np.float32).astype(ml_dtypes.bfloat16).astype(np.float64), axis, -1)
    blocks = v.reshape(v.shape[:-1] + (-1, 32))
    amax = np.abs(blocks).max(-1, keepdims=True)
    byte = np.maximum(np.where(amax > 0, np.frexp(amax)[1] - 1 + 127, 0) - down, 1)
    scale = np.exp2(byte - 127.0)
    codes = (blocks / scale).astype(np.float32).astype(dtype).astype(np.float64)
    return np.moveaxis((codes * scale).reshape(v.shape), -1, axis)


WIDE = False


def mx_kscale(k):
    if not WIDE:
        return np.ones(k)
    levels = np.array([10, -10, 5, -5, 0])
    if k % 512:
        return np.exp2(np.random.permutation(np.resize(levels, k // 32))).repeat(32)
    a = np.empty((k // 512, 16))
    for p in range(k // 512):
        a[p, :8] = np.random.permutation(np.resize(levels, 8))
        for g in range(8):
            far = levels[np.abs(levels - a[p, g]) >= 10]
            a[p, g + 8] = far[np.random.randint(len(far))]
    return np.exp2(a.ravel()).repeat(32)


def f64(x):
    return np.asarray(x).astype(np.float64)


def striped(idx):
    return np.tile(idx.reshape(-1, 16).T, (8, 1)).astype(np.uint16)


def unstriped(offs):
    return offs[:16].T.reshape(-1).astype(np.int64)


def striped8(idx):
    return np.concatenate([x.reshape(-1, 16).T for x in idx]).astype(np.uint16)


def runs(offs, k):
    lists = np.stack([offs[16 * r : 16 * r + 16].T.reshape(-1) for r in range(8)]).astype(np.int64)
    return lists[np.arange(k) % 512 // 64]


def pack_weight(w):
    k, n = w.shape
    w = f64(np.asarray(w, np.float32).astype(ml_dtypes.bfloat16)).reshape(k // 32, 32, n)
    amax = np.abs(w).max(1)
    byte = np.clip(np.where(amax > 0, np.frexp(amax)[1] - 1 + 127 - 7, 1), 1, 254)
    scaled = (w * np.exp2(127.0 - byte)[:, None, :]).reshape(k, n).astype(np.float32)
    words = np.ascontiguousarray(scaled.reshape(k // 512, 128, 4, n).transpose(0, 1, 3, 2)).astype(ml_dtypes.float8_e4m3fn).view(np.uint8)
    return words, np.ascontiguousarray(byte.astype(np.uint8).reshape(k // 512, 16, n))


def unpack_weight(words, scales):
    g, p, n, _ = words.shape
    vals = np.ascontiguousarray(words).view(ml_dtypes.float8_e4m3fn).astype(np.float64) * np.repeat(np.exp2(scales.astype(np.float64) - 127.0), 8, axis=1)[..., None]
    return vals.transpose(0, 1, 3, 2).reshape(g * 512, n)


E2M1 = np.array([0.0, 0.5, 1.0, 1.5, 2.0, 3.0, 4.0, 6.0, -0.0, -0.5, -1.0, -1.5, -2.0, -3.0, -4.0, -6.0])


def pack_fp4(w):
    k, n = w.shape
    w = f64(np.asarray(w, np.float32).astype(ml_dtypes.bfloat16)).reshape(k // 32, 32, n)
    amax = np.abs(w).max(1)
    mant, ex = np.frexp(amax / 6.0)
    byte = np.clip(np.where(amax > 0, np.where(mant > 0.5, ex, ex - 1) + 127, 1), 1, 254)
    scaled = (w * np.exp2(127.0 - byte)[:, None, :]).reshape(k, n).astype(np.float32)
    c = np.ascontiguousarray(scaled.reshape(k // 512, 128, 4, n).transpose(0, 1, 3, 2)).astype(ml_dtypes.float4_e2m1fn).view(np.uint8) & 0xF
    words = (c[..., 0::2] | (c[..., 1::2] << 4)).reshape(k // 512, 128, 2 * n)
    return np.ascontiguousarray(words), np.ascontiguousarray(byte.astype(np.uint8).reshape(k // 512, 16, n))


def unpack_fp4(words, scales):
    g, _, n = scales.shape
    words = np.ascontiguousarray(words).reshape(g, 128, n, 2)
    nib = np.empty((g, 128, n, 4), np.uint8)
    nib[..., 0::2] = words & 0xF
    nib[..., 1::2] = words >> 4
    vals = E2M1[nib] * np.repeat(np.exp2(scales.astype(np.float64) - 127.0), 8, axis=1)[..., None]
    return vals.transpose(0, 1, 3, 2).reshape(g * 512, n)


def planes(y):
    n, m = y.shape
    v = y.astype(np.float32).astype(ml_dtypes.bfloat16).astype(np.float64).reshape(n // 32, 32, m)
    top = np.abs(v).max(1)
    byte = np.clip(np.where(top > 0, np.frexp(top)[1] - 1 + 127 - 7, 1), 1, 254)
    codes = (v * np.exp2(127.0 - byte)[:, None, :]).reshape(n, m).astype(np.float32).astype(ml_dtypes.float8_e4m3fn).view(np.uint8)
    words = codes.reshape(n // 512, 128, 4, m).transpose(0, 1, 3, 2)
    return np.ascontiguousarray(words), np.ascontiguousarray(byte.astype(np.uint8).reshape(n // 512, 16, m))


K, T, S, N, H = 512, 2048, 512, 512, 512


def setup_inputs():
    n = np.random.standard_normal
    s = mx_kscale(K)[:, None]
    u = mx_kscale(H)
    packed_xT = pack_weight(n((K, T)) * s)
    packed_w1 = pack_fp4(n((K, H)) / np.sqrt(K) / s)
    packed_w2 = pack_fp4(n((H, N)) / np.sqrt(H) / u[:, None])
    return {
        "x_words": packed_xT[0],
        "x_scales": packed_xT[1],
        "w1_words": packed_w1[0],
        "w1_scales": packed_w1[1],
        "gn": (np.random.uniform(0.5, 1.5, (H, 1)) * u[:, None]).astype(np.float32),
        "w2_words": packed_w2[0],
        "w2_scales": packed_w2[1],
        "offs": striped(np.random.permutation(T)[:S]),
        "p1": striped8(np.stack([np.random.permutation(S) for _ in range(8)])),
        "p2": striped8(np.stack([np.random.permutation(S) for _ in range(8)])),
        "q1": striped8(np.stack([np.random.permutation(S) for _ in range(8)])),
        "q2": striped8(np.stack([np.random.permutation(S) for _ in range(8)])),
    }


def reference(x_words, x_scales, w1_words, w1_scales, gn, w2_words, w2_scales, offs, p1, p2, q1, q2):
    xq = unpack_weight(x_words, x_scales)[:, unstriped(offs)]
    y = unpack_fp4(w1_words, w1_scales).T @ xq
    h = y + 0.5 * (np.tanh(y[np.arange(H)[:, None], runs(p1, H)] - y) + np.tanh(y[np.arange(H)[:, None], runs(p2, H)] - y))
    z = f64(gn) * (h + 0.5 * (np.tanh(h[np.arange(H)[:, None], runs(q1, H)] - h) + np.tanh(h[np.arange(H)[:, None], runs(q2, H)] - h)))
    out_0 = unpack_fp4(w2_words, w2_scales).T @ mxq(z, 0, "e4m3")
    return (out_0,) + planes(out_0)

@@ -1,0 +1,193 @@
+from contextlib import ExitStack
+
+import concourse.mybir as mybir
+
+K, T, S, H, N = 512, 2048, 512, 512, 512
+FLOPS = 2 * K * H * S + 2 * H * N * S
+
+F32 = mybir.dt.float32
+BF16 = mybir.dt.bfloat16
+I32 = mybir.dt.int32
+U32 = mybir.dt.uint32
+U16 = mybir.dt.uint16
+U8 = mybir.dt.uint8
+FP8X4 = mybir.dt.float8_e4m3fn_x4
+FP4X4 = mybir.dt.float4_e2m1fn_x4
+ADD = mybir.AluOpType.add
+SUB = mybir.AluOpType.subtract
+MULT = mybir.AluOpType.mult
+COPY = mybir.ActivationFunctionType.Copy
+TANH = mybir.ActivationFunctionType.Tanh
+
+P = 128
+PACK = 4
+HALF = 256
+BLK = 128
+CHUNKS = ((0, 256), (256, 128), (384, 128))
+
+
+def load_scales(queues, tile, rows):
+    for q in range(4):
+        queues[q].dma_start(tile[32 * q : 32 * q + 4, :].bitcast(I32), rows[4 * q : 4 * q + 4, :].bitcast(I32))
+
+
+def deal_columns(nc, pool, name, words, scales):
+    dealt_words = pool.tile([P, 2 * H], U8, name=name + "_dw", align_bytes=64)
+    dealt_scales = pool.tile([P, H], U8, name=name + "_ds", align_bytes=64)
+    nc.vector.tensor_copy(
+        dealt_words[:].rearrange("p (t m b) -> p m t b", t=PACK, b=2),
+        words[:].rearrange("p (m t b) -> p m t b", t=PACK, b=2),
+    )
+    nc.vector.tensor_copy(
+        dealt_scales[:].rearrange("p (t m) -> p m t", t=PACK),
+        scales[:].rearrange("p (m t) -> p m t", t=PACK),
+    )
+    return dealt_words, dealt_scales
+
+
+def interleave(engine_copy, dst, src):
+    engine_copy(
+        dst.rearrange("p (c i t) -> p c t i", i=4, t=PACK),
+        src.rearrange("p t (c i) -> p c t i", i=4),
+    )
+
+
+def tile_picked_coupled_none_po_kernel(
+    tc, x_words, x_scales, w1_words, w1_scales, gn, w2_words, w2_scales, offs, p1, p2, q1, q2, out_0, out_1, out_2
+):
+    nc = tc.nc
+    with ExitStack() as ctx:
+        lists = ctx.enter_context(tc.tile_pool(name="lists", bufs=1))
+        sb = ctx.enter_context(tc.tile_pool(name="sb", bufs=1))
+        ps = ctx.enter_context(tc.psum_pool(name="ps", bufs=1))
+
+        offs_t = lists.tile([P, S // 16], U16, name="offs_t")
+        p_t = [lists.tile([P, S // 16], U16, name=f"p_t{i}") for i in range(2)]
+        q_t = [lists.tile([P, S // 16], U16, name=f"q_t{i}") for i in range(2)]
+
+        xw = sb.tile([P, T], U32, name="xw", align_bytes=64)
+        xs = sb.tile([P, T], U8, name="xs", align_bytes=64)
+        w1w = sb.tile([P, 2 * H], U8, name="w1w", align_bytes=64)
+        w1s = sb.tile([P, H], U8, name="w1s", align_bytes=64)
+        w2w = sb.tile([P, 2 * N], U8, name="w2w", align_bytes=64)
+        w2s = sb.tile([P, N], U8, name="w2s", align_bytes=64)
+        gain = sb.tile([P, PACK], F32, name="gain")
+
+        nc.vector.memset(xs[:].bitcast(I32), 0)
+        nc.gpsimd.memset(w1s[:].bitcast(I32), 0)
+        nc.sync.dma_start(offs_t[:], offs)
+        nc.scalar.dma_start(w1w[:].bitcast(I32), w1_words[0].bitcast(I32))
+        nc.sync.dma_start(p_t[0][:], p1)
+        nc.sync.dma_start(p_t[1][:], p2)
+        nc.sync.dma_start(xw[:].bitcast(I32), x_words[0].rearrange("p n t -> p (n t)").bitcast(I32))
+        load_scales([nc.gpsimd, nc.gpsimd, nc.gpsimd, nc.scalar], w1s, w1_scales[0])
+        load_scales([nc.scalar] * 4, xs, x_scales[0])
+        nc.sync.dma_start(q_t[0][:], q1)
+        nc.sync.dma_start(q_t[1][:], q2)
+        nc.gpsimd.dma_start(w2w[:].bitcast(I32), w2_words[0].bitcast(I32))
+        nc.gpsimd.memset(w2s[:].bitcast(I32), 0)
+        load_scales([nc.sync] * 4, w2s, w2_scales[0])
+        nc.gpsimd.dma_start(gain[:], gn.rearrange("(p t) o -> p (t o)", t=PACK))
+
+        xgs = sb.tile([P, S], U8, name="xgs", align_bytes=64)
+        nc.vector.tensor_copy(xgs[:], xs[:].indirect(offs_t[:]))
+        w1dw, w1ds = deal_columns(nc, sb, "w1", w1w, w1s)
+        xg = sb.tile([P, S], U32, name="xg", align_bytes=64)
+        for a in range(2):
+            nc.vector.tensor_copy(xg[:, HALF * a : HALF * (a + 1)], xw[:].indirect(offs_t[:, 16 * a : 16 * (a + 1)]))
+
+        def product(bank, dw, ds, t, codes, scales):
+            nc.tensor.matmul_mx(
+                out=bank,
+                lhsT=dw[:, 2 * P * t : 2 * P * (t + 1)].bitcast(FP4X4),
+                lhsT_scale=ds[:, P * t : P * (t + 1)],
+                rhs=codes.bitcast(FP8X4),
+                rhs_scale=scales,
+                start=True,
+                stop=True,
+            )
+
+        yw = [sb.tile([P, S], F32, name=f"yw{t}") for t in range(PACK)]
+        yp = [sb.tile([P, S], F32, name=f"yp{t}") for t in range(PACK)]
+        for a in range(2):
+            cols = slice(HALF * a, HALF * (a + 1))
+            bank = ps.tile([P, HALF], F32, name=f"y0_{a}")
+            product(bank[:], w1dw, w1ds, 0, xg[:, cols], xgs[:, cols])
+            nc.scalar.activation(yw[0][:, cols], bank[:], COPY, scale=2.0)
+            if a == 0:
+                nc.vector.tensor_scalar(yp[0][:, cols], bank[:], 2.0, None, MULT)
+            else:
+                nc.scalar.activation(yp[0][:, cols], bank[:], COPY, scale=2.0)
+        for t in range(1, PACK):
+            bank = ps.tile([P, S], F32, name=f"y{t}")
+            product(bank[:], w1dw, w1ds, t, xg[:], xgs[:])
+            nc.scalar.activation(yw[t][:], bank[:], COPY, scale=2.0)
+            nc.scalar.activation(yp[t][:], bank[:], COPY, scale=2.0)
+
+        w2dw, w2ds = deal_columns(nc, sb, "w2", w2w, w2s)
+        half_gain = sb.tile([P, PACK], F32, name="half_gain")
+        nc.vector.tensor_scalar(half_gain[:], gain[:], 0.5, None, MULT)
+
+        hw = [sb.tile([P, S], F32, name=f"hw{t}") for t in range(PACK)]
+        hp = [sb.tile([P, S], F32, name=f"hp{t}") for t in range(PACK)]
+        gh = [sb.tile([P, S], F32, name=f"gh{t}") for t in range(PACK)]
+        for t in range(PACK):
+            pulls = []
+            for i in range(2):
+                d = sb.tile([P, S], F32, name=f"d1_{t}_{i}")
+                for a in range(2):
+                    cols = slice(HALF * a, HALF * (a + 1))
+                    nc.vector.tensor_tensor(
+                        d[:, cols], yw[t][:].indirect(p_t[i][:, 16 * a : 16 * (a + 1)]), yp[t][:, cols], SUB
+                    )
+                pull = sb.tile([P, S], F32, name=f"t1_{t}_{i}")
+                nc.scalar.activation(pull[:], d[:], TANH, scale=0.5)
+                pulls.append(pull)
+            u = sb.tile([P, S], F32, name=f"u{t}")
+            nc.vector.tensor_tensor(u[:], pulls[0][:], yp[t][:], ADD)
+            nc.vector.tensor_tensor(hw[t][:], pulls[1][:], u[:], ADD)
+            nc.scalar.copy(hp[t][:], hw[t][:])
+            nc.scalar.activation(gh[t][:], hw[t][:], COPY, scale=half_gain[:, t : t + 1])
+
+        ow = sb.tile([P, S], U32, name="ow", align_bytes=64)
+        osc = sb.tile([P, S], U8, name="osc", align_bytes=64)
+        out_rows = out_0.rearrange("(p t) j -> p t j", t=PACK)
+        out_words = out_1[0].rearrange("p n t -> p (n t)").bitcast(I32)
+        for c, (c0, w) in enumerate(CHUNKS):
+            last = c == len(CHUNKS) - 1
+            cols = slice(c0, c0 + w)
+            zb = sb.tile([P, PACK, w], BF16, name=f"zb{c}")
+            for t in range(PACK):
+                d = sb.tile([P, 2, w], F32, name=f"d2_{c}_{t}")
+                for i in range(2):
+                    nc.vector.tensor_tensor(
+                        d[:, i, :], hw[t][:].indirect(q_t[i][:, c0 // 16 : (c0 + w) // 16]), hp[t][:, cols], SUB
+                    )
+                pull = sb.tile([P, 2, w], F32, name=f"t2_{c}_{t}")
+                nc.scalar.activation(pull[:], d[:], TANH, scale=0.5)
+                u = sb.tile([P, w], F32, name=f"u2_{c}_{t}")
+                g = half_gain[:, t : t + 1]
+                nc.vector.scalar_tensor_tensor(u[:], pull[:, 0, :], g, gh[t][:, cols], MULT, ADD)
+                nc.vector.scalar_tensor_tensor(zb[:, t, :], pull[:, 1, :], g, u[:], MULT, ADD)
+            zi = sb.tile([P, PACK * w], BF16, name=f"zi{c}", align_bytes=64)
+            interleave(nc.vector.tensor_copy if last else nc.scalar.copy, zi[:], zb[:])
+            zc = sb.tile([P, w], U32, name=f"zc{c}", align_bytes=64)
+            zs = sb.tile([P, w], U8, name=f"zs{c}", align_bytes=64)
+            nc.vector.quantize_mx(out=zc[:].bitcast(FP8X4), scales=zs[:], in_=zi[:])
+            for b0 in range(0, w, BLK):
+                j0 = c0 + b0
+                blk = slice(j0, j0 + BLK)
+                bank = ps.tile([P, PACK, BLK], F32, name=f"o{j0}", tag=f"o{(j0 // BLK) % 3}")
+                for t in range(PACK):
+                    product(bank[:, t, :], w2dw, w2ds, t, zc[:, b0 : b0 + BLK], zs[:, b0 : b0 + BLK])
+                oi = sb.tile([P, PACK * BLK], BF16, name=f"oi{j0}", align_bytes=64)
+                copy = nc.vector.tensor_copy if last else nc.scalar.copy
+                copy(oi[:].rearrange("p (j t) -> p j t", t=PACK), bank[:].rearrange("p t j -> p j t"))
+                of = sb.tile([P, PACK, BLK], F32, name=f"of{j0}")
+                nc.scalar.copy(of[:], bank[:])
+                nc.vector.quantize_mx(out=ow[:, blk].bitcast(FP8X4), scales=osc[:, blk], in_=oi[:])
+                nc.sync.dma_start(out_rows[:, :, blk], of[:])
+                nc.sync.dma_start(out_words[:, blk], ow[:, blk].bitcast(I32))
+        for q in range(4):
+            queue = nc.scalar if q % 2 else nc.sync
+            queue.dma_start(out_2[0][4 * q : 4 * q + 4, :].bitcast(I32), osc[32 * q : 32 * q + 4, :].bitcast(I32))

@@ -1,6 +1,7 @@
 from contextlib import ExitStack
 
 import concourse.mybir as mybir
+from concourse.masks import make_identity
 
 K, T, S, H, N = 512, 2048, 512, 512, 512
 FLOPS = 2 * K * H * S + 2 * H * N * S
@@ -32,8 +33,8 @@ def load_scales(queues, tile, rows):
 
 
 def deal_columns(nc, pool, name, words, scales):
-    dealt_words = pool.tile([P, 2 * H], U8, name=name + "_dw", align_bytes=64)
-    dealt_scales = pool.tile([P, H], U8, name=name + "_ds", align_bytes=64)
+    dealt_words = pool.tile([P, 2 * H], U8, name=name + "_dw", tag="yw3", align_bytes=64)
+    dealt_scales = pool.tile([P, H], U8, name=name + "_ds", tag="yw2", align_bytes=64)
     nc.vector.tensor_copy(
         dealt_words[:].rearrange("p (t m b) -> p m t b", t=PACK, b=2),
         words[:].rearrange("p (m t b) -> p m t b", t=PACK, b=2),
@@ -66,32 +67,43 @@ def tile_picked_coupled_none_po_kernel(
         q_t = [lists.tile([P, S // 16], U16, name=f"q_t{i}") for i in range(2)]
 
         xw = sb.tile([P, T], U32, name="xw", align_bytes=64)
+        xs_rows = sb.tile([P, T], U8, name="xs_rows", tag="early", align_bytes=64)
         xs = sb.tile([P, T], U8, name="xs", align_bytes=64)
-        w1w = sb.tile([P, 2 * H], U8, name="w1w", align_bytes=64)
-        w1s = sb.tile([P, H], U8, name="w1s", align_bytes=64)
-        w2w = sb.tile([P, 2 * N], U8, name="w2w", align_bytes=64)
-        w2s = sb.tile([P, N], U8, name="w2s", align_bytes=64)
-        gain = sb.tile([P, PACK], F32, name="gain")
+        ww = sb.tile([P, 2 * H], U8, name="ww", align_bytes=64)
+        ident = sb.tile([P, P], F32, name="ident")
 
+        w1dw = sb.tile([P, 2 * H], U8, name="w1dw", align_bytes=64)
+        w1ds = sb.tile([P, H], U8, name="w1ds", align_bytes=64)
+        w1s = sb.tile([P, H], U8, name="w1s", tag="raw_scales", align_bytes=64)
         nc.vector.memset(xs[:].bitcast(I32), 0)
-        nc.gpsimd.memset(w1s[:].bitcast(I32), 0)
+        nc.vector.memset(w1ds[:].bitcast(I32), 0)
         nc.sync.dma_start(offs_t[:], offs)
-        nc.scalar.dma_start(w1w[:].bitcast(I32), w1_words[0].bitcast(I32))
+        nc.scalar.dma_start(ww[:].bitcast(I32), w1_words[0].bitcast(I32))
+        load_scales([nc.sync, nc.scalar, nc.sync, nc.scalar], xs_rows, x_scales[0])
+        nc.sync.dma_start(xw[:].bitcast(I32), x_words[0].rearrange("p n t -> p (n t)").bitcast(I32))
+        load_scales([nc.scalar, nc.scalar, nc.scalar, nc.scalar], w1s, w1_scales[0])
         nc.sync.dma_start(p_t[0][:], p1)
         nc.sync.dma_start(p_t[1][:], p2)
-        nc.sync.dma_start(xw[:].bitcast(I32), x_words[0].rearrange("p n t -> p (n t)").bitcast(I32))
-        load_scales([nc.gpsimd, nc.gpsimd, nc.gpsimd, nc.scalar], w1s, w1_scales[0])
-        load_scales([nc.scalar] * 4, xs, x_scales[0])
         nc.sync.dma_start(q_t[0][:], q1)
         nc.sync.dma_start(q_t[1][:], q2)
-        nc.gpsimd.dma_start(w2w[:].bitcast(I32), w2_words[0].bitcast(I32))
-        nc.gpsimd.memset(w2s[:].bitcast(I32), 0)
-        load_scales([nc.sync] * 4, w2s, w2_scales[0])
-        nc.gpsimd.dma_start(gain[:], gn.rearrange("(p t) o -> p (t o)", t=PACK))
+        make_identity(nc, ident[:])
+        warm = sb.tile([P, 1], F32, name="warm")
+        nc.scalar.activation(warm[:], ident[:, 0:1], TANH)
 
+        def deal_runs(dealt, raw):
+            nc.vector.tensor_copy(
+                dealt.bitcast(I32).rearrange("p (t g x) -> p t g x", t=PACK, g=8),
+                raw.bitcast(I32).rearrange("p (g t x) -> p t g x", t=PACK, g=8),
+            )
+
+        for q in range(4):
+            rows = slice(32 * q, 32 * q + 4)
+            nc.vector.tensor_copy(xs[rows, :].bitcast(I32), xs_rows[rows, :].bitcast(I32))
+        deal_runs(w1dw[:], ww[:])
+        for q in range(4):
+            deal_runs(w1ds[32 * q : 32 * q + 4, :], w1s[32 * q : 32 * q + 4, :])
         xgs = sb.tile([P, S], U8, name="xgs", align_bytes=64)
         nc.vector.tensor_copy(xgs[:], xs[:].indirect(offs_t[:]))
-        w1dw, w1ds = deal_columns(nc, sb, "w1", w1w, w1s)
         xg = sb.tile([P, S], U32, name="xg", align_bytes=64)
         for a in range(2):
             nc.vector.tensor_copy(xg[:, HALF * a : HALF * (a + 1)], xw[:].indirect(offs_t[:, 16 * a : 16 * (a + 1)]))
@@ -107,87 +119,161 @@ def tile_picked_coupled_none_po_kernel(
                 stop=True,
             )
 
-        yw = [sb.tile([P, S], F32, name=f"yw{t}") for t in range(PACK)]
+        def turned_sum(out, terms):
+            for n, term in enumerate(terms):
+                nc.tensor.matmul(out, term, ident[:], start=n == 0, stop=n == len(terms) - 1, is_transpose=True)
+
+        def new_bank(n, name):
+            return ps.tile([P, 512], F32, name=name, tag=f"bank{n}")
+
+        yw = [sb.tile([P, S], F32, name=f"yw{t}", tag=f"yw{t}", align_bytes=64) for t in range(PACK)]
         yp = [sb.tile([P, S], F32, name=f"yp{t}") for t in range(PACK)]
         for a in range(2):
             cols = slice(HALF * a, HALF * (a + 1))
-            bank = ps.tile([P, HALF], F32, name=f"y0_{a}")
-            product(bank[:], w1dw, w1ds, 0, xg[:, cols], xgs[:, cols])
-            nc.scalar.activation(yw[0][:, cols], bank[:], COPY, scale=2.0)
+            bank = new_bank(a, f"y0_{a}")[:, :HALF]
+            product(bank, w1dw, w1ds, 0, xg[:, cols], xgs[:, cols])
+            nc.scalar.activation(yw[0][:, cols], bank, COPY, scale=2.0)
             if a == 0:
-                nc.vector.tensor_scalar(yp[0][:, cols], bank[:], 2.0, None, MULT)
+                nc.vector.tensor_scalar(yp[0][:, cols], bank, 2.0, None, MULT)
             else:
-                nc.scalar.activation(yp[0][:, cols], bank[:], COPY, scale=2.0)
+                nc.scalar.activation(yp[0][:, cols], bank, COPY, scale=2.0)
+        y_banks = {}
         for t in range(1, PACK):
-            bank = ps.tile([P, S], F32, name=f"y{t}")
-            product(bank[:], w1dw, w1ds, t, xg[:], xgs[:])
-            nc.scalar.activation(yw[t][:], bank[:], COPY, scale=2.0)
-            nc.scalar.activation(yp[t][:], bank[:], COPY, scale=2.0)
+            y_banks[t] = new_bank(1 + t, f"y{t}")
+            product(y_banks[t][:], w1dw, w1ds, t, xg[:], xgs[:])
 
-        w2dw, w2ds = deal_columns(nc, sb, "w2", w2w, w2s)
-        half_gain = sb.tile([P, PACK], F32, name="half_gain")
-        nc.vector.tensor_scalar(half_gain[:], gain[:], 0.5, None, MULT)
+        ws = sb.tile([P, H], U8, name="ws", tag="raw_scales", align_bytes=64)
+        nc.gpsimd.memset(ws[:].bitcast(I32), 0)
+        nc.sync.dma_start(ww[:].bitcast(I32), w2_words[0].bitcast(I32))
+        load_scales([nc.sync] * 4, ws, w2_scales[0])
+        gain_rows = sb.tile([P, H], F32, name="gain_rows", tag="early", align_bytes=64)
+        nc.sync.dma_start(gain_rows[:], gn.rearrange("f o -> (f o)").partition_broadcast(P))
+
+        def pulls(window, plain, pair, c0, w, name):
+            d = sb.tile([P, 2, w], F32, name="d" + name, tag="d", bufs=3)
+            for i in range(2):
+                nc.vector.tensor_tensor(
+                    d[:, i, :], window[:].indirect(pair[i][:, c0 // 16 : (c0 + w) // 16]), plain[:, c0 : c0 + w], SUB
+                )
+            pull = sb.tile([P, 2, w], F32, name="pull" + name, tag="pull", bufs=4)
+            nc.scalar.activation(pull[:], d[:], TANH, scale=0.5)
+            return pull
 
         hw = [sb.tile([P, S], F32, name=f"hw{t}") for t in range(PACK)]
         hp = [sb.tile([P, S], F32, name=f"hp{t}") for t in range(PACK)]
-        gh = [sb.tile([P, S], F32, name=f"gh{t}") for t in range(PACK)]
-        for t in range(PACK):
-            pulls = []
-            for i in range(2):
-                d = sb.tile([P, S], F32, name=f"d1_{t}_{i}")
-                for a in range(2):
-                    cols = slice(HALF * a, HALF * (a + 1))
-                    nc.vector.tensor_tensor(
-                        d[:, cols], yw[t][:].indirect(p_t[i][:, 16 * a : 16 * (a + 1)]), yp[t][:, cols], SUB
-                    )
-                pull = sb.tile([P, S], F32, name=f"t1_{t}_{i}")
-                nc.scalar.activation(pull[:], d[:], TANH, scale=0.5)
-                pulls.append(pull)
-            u = sb.tile([P, S], F32, name=f"u{t}")
-            nc.vector.tensor_tensor(u[:], pulls[0][:], yp[t][:], ADD)
-            nc.vector.tensor_tensor(hw[t][:], pulls[1][:], u[:], ADD)
-            nc.scalar.copy(hp[t][:], hw[t][:])
-            nc.scalar.activation(gh[t][:], hw[t][:], COPY, scale=half_gain[:, t : t + 1])
+        ht = [sb.tile([P, S], F32, name=f"ht{t}") for t in range(PACK)]
+        ht_banks = {}
+        zt_banks = {}
+
+        def y_window(t):
+            nc.scalar.activation(yw[t][:], y_banks[t][:], COPY, scale=2.0)
+            if t > 1:
+                nc.sync.dma_start(yp[t][:], yw[t][:])
+
+        def step1(t, a):
+            if a == 0:
+                ht_banks[t] = new_bank(5 + t % 2, f"ht_bank{t}")
+            pull = pulls(yw[t], yp[t], p_t, HALF * a, HALF, f"1_{t}_{a}")
+            for b0 in range(0, HALF, BLK):
+                blk = slice(HALF * a + b0, HALF * a + b0 + BLK)
+                sub = slice(b0, b0 + BLK)
+                turned_sum(ht_banks[t][:, blk], [yp[t][:, blk], pull[:, 0, sub], pull[:, 1, sub]])
+
+        def h_turned(t):
+            nc.scalar.copy(ht[t][:], ht_banks[t][:])
+
+        def h_window(t):
+            bank = new_bank(0 if t % 2 else 7, f"h_bank{t}")
+            for j0 in range(0, S, BLK):
+                turned_sum(bank[:, j0 : j0 + BLK], [ht[t][:, j0 : j0 + BLK]])
+            nc.scalar.copy(hw[t][:], bank[:])
+            if t >= 3:
+                nc.scalar.copy(hp[t][:], bank[:])
+            else:
+                nc.sync.dma_start(hp[t][:], hw[t][:])
+
+        def step2(c, t):
+            c0, w = CHUNKS[c]
+            pull = pulls(hw[t], hp[t], q_t, c0, w, f"2_{c}_{t}")
+            for j0 in range(c0, c0 + w, BLK):
+                if t == 0:
+                    zt_banks[j0] = new_bank(1 + j0 // BLK, f"zt_bank{j0}")
+                sub = slice(j0 - c0, j0 - c0 + BLK)
+                turned_sum(
+                    zt_banks[j0][:].rearrange("j (g t r) -> j t g r", t=PACK, g=8)[:, t],
+                    [hp[t][:, j0 : j0 + BLK], pull[:, 0, sub], pull[:, 1, sub]],
+                )
 
         ow = sb.tile([P, S], U32, name="ow", align_bytes=64)
         osc = sb.tile([P, S], U8, name="osc", align_bytes=64)
         out_rows = out_0.rearrange("(p t) j -> p t j", t=PACK)
         out_words = out_1[0].rearrange("p n t -> p (n t)").bitcast(I32)
-        for c, (c0, w) in enumerate(CHUNKS):
-            last = c == len(CHUNKS) - 1
-            cols = slice(c0, c0 + w)
-            zb = sb.tile([P, PACK, w], BF16, name=f"zb{c}")
-            for t in range(PACK):
-                d = sb.tile([P, 2, w], F32, name=f"d2_{c}_{t}")
-                for i in range(2):
-                    nc.vector.tensor_tensor(
-                        d[:, i, :], hw[t][:].indirect(q_t[i][:, c0 // 16 : (c0 + w) // 16]), hp[t][:, cols], SUB
-                    )
-                pull = sb.tile([P, 2, w], F32, name=f"t2_{c}_{t}")
-                nc.scalar.activation(pull[:], d[:], TANH, scale=0.5)
-                u = sb.tile([P, w], F32, name=f"u2_{c}_{t}")
-                g = half_gain[:, t : t + 1]
-                nc.vector.scalar_tensor_tensor(u[:], pull[:, 0, :], g, gh[t][:, cols], MULT, ADD)
-                nc.vector.scalar_tensor_tensor(zb[:, t, :], pull[:, 1, :], g, u[:], MULT, ADD)
-            zi = sb.tile([P, PACK * w], BF16, name=f"zi{c}", align_bytes=64)
-            interleave(nc.vector.tensor_copy if last else nc.scalar.copy, zi[:], zb[:])
-            zc = sb.tile([P, w], U32, name=f"zc{c}", align_bytes=64)
-            zs = sb.tile([P, w], U8, name=f"zs{c}", align_bytes=64)
+        zts = {j0: sb.tile([P, H], BF16, name=f"zt{j0}") for j0 in range(0, S, BLK)}
+
+        def scale_z(j0, pick):
+            nc.vector.scalar_tensor_tensor(pick(zts[j0][:]), pick(zt_banks[j0][:]), 0.5, pick(gain_rows[:]), MULT, MULT)
+
+        def finish(j0):
+            n = j0 // BLK
+            last = j0 + BLK == S
+            blk = slice(j0, j0 + BLK)
+            zt = zts[j0]
+            bank = new_bank(5 + n % 2, f"z_bank{j0}")
+            words = zt[:].bitcast(F32).rearrange("j (p u) -> j u p", u=2)
+            for u in range(2):
+                turned_sum(bank[:, BLK * u : BLK * (u + 1)], [words[:, u, :]])
+            zi = sb.tile([P, PACK * BLK], BF16, name=f"zi{j0}", align_bytes=64)
+            nc.scalar.copy(
+                zi[:].bitcast(F32).rearrange("p (j u) -> p j u", u=2),
+                bank[:, : 2 * BLK].rearrange("p (u j) -> p j u", u=2),
+            )
+            zc = sb.tile([P, BLK], U32, name=f"zc{j0}", align_bytes=64)
+            zs = sb.tile([P, BLK], U8, name=f"zs{j0}", align_bytes=64)
             nc.vector.quantize_mx(out=zc[:].bitcast(FP8X4), scales=zs[:], in_=zi[:])
-            for b0 in range(0, w, BLK):
-                j0 = c0 + b0
-                blk = slice(j0, j0 + BLK)
-                bank = ps.tile([P, PACK, BLK], F32, name=f"o{j0}", tag=f"o{(j0 // BLK) % 3}")
-                for t in range(PACK):
-                    product(bank[:, t, :], w2dw, w2ds, t, zc[:, b0 : b0 + BLK], zs[:, b0 : b0 + BLK])
-                oi = sb.tile([P, PACK * BLK], BF16, name=f"oi{j0}", align_bytes=64)
-                copy = nc.vector.tensor_copy if last else nc.scalar.copy
-                copy(oi[:].rearrange("p (j t) -> p j t", t=PACK), bank[:].rearrange("p t j -> p j t"))
-                of = sb.tile([P, PACK, BLK], F32, name=f"of{j0}")
-                nc.scalar.copy(of[:], bank[:])
-                nc.vector.quantize_mx(out=ow[:, blk].bitcast(FP8X4), scales=osc[:, blk], in_=oi[:])
-                nc.sync.dma_start(out_rows[:, :, blk], of[:])
-                nc.sync.dma_start(out_words[:, blk], ow[:, blk].bitcast(I32))
+            bank = new_bank(0 if n % 2 else 7, f"o_bank{j0}")
+            for t in range(PACK):
+                product(bank[:, BLK * t : BLK * (t + 1)], w2dw, w2ds, t, zc[:], zs[:])
+            oi = sb.tile([P, PACK * BLK], BF16, name=f"oi{j0}", align_bytes=64)
+            copy = nc.vector.tensor_copy if last else nc.scalar.copy
+            copy(oi[:].rearrange("p (j t) -> p j t", t=PACK), bank[:].rearrange("p (t j) -> p j t", t=PACK))
+            of = sb.tile([P, PACK, BLK], F32, name=f"of{j0}")
+            nc.scalar.copy(of[:], bank[:].rearrange("p (t j) -> p t j", t=PACK))
+            nc.vector.quantize_mx(out=ow[:, blk].bitcast(FP8X4), scales=osc[:, blk], in_=oi[:])
+            nc.sync.dma_start(out_rows[:, :, blk], of[:])
+            nc.sync.dma_start(out_words[:, blk], ow[:, blk].bitcast(I32))
+
+        y_window(1)
+        step1(0, 0)
+        nc.scalar.activation(yp[1][:], y_banks[1][:], COPY, scale=2.0)
+        step1(0, 1)
+        y_window(2)
+        for t in range(1, PACK):
+            step1(t, 0)
+            h_turned(t - 1)
+            if t == 1:
+                y_window(3)
+            step1(t, 1)
+            h_window(t - 1)
+        step2(0, 0)
+        h_turned(3)
+        step2(0, 1)
+        h_window(3)
+        step2(1, 0)
+        step2(1, 1)
+        w2dw, w2ds = deal_columns(nc, sb, "w2", ww, ws)
+        step2(0, 2)
+        step2(0, 3)
+        for j0 in (0, BLK):
+            scale_z(j0, lambda ap: ap)
+            finish(j0)
+        step2(1, 2)
+        step2(1, 3)
+        scale_z(2 * BLK, lambda ap: ap)
+        finish(2 * BLK)
+        for t in range(PACK):
+            step2(2, t)
+        scale_z(3 * BLK, lambda ap: ap)
+        finish(3 * BLK)
         for q in range(4):
             queue = nc.scalar if q % 2 else nc.sync
             queue.dma_start(out_2[0][4 * q : 4 * q + 4, :].bitcast(I32), osc[32 * q : 32 * q + 4, :].bitcast(I32))

@@ -24,7 +24,9 @@ P = 128
 PACK = 4
 HALF = 256
 BLK = 128
-CHUNKS = ((0, 256), (256, 128), (384, 128))
+ROW_STORES = {1: 0, 3: 256}
+WORD_STORES = {2: 0, 3: 384}
+CHUNKS = ((0, 384), (384, 128))
 
 
 def load_scales(queues, tile, rows):
@@ -34,7 +36,7 @@ def load_scales(queues, tile, rows):
 
 def deal_columns(nc, pool, name, words, scales):
     dealt_words = pool.tile([P, 2 * H], U8, name=name + "_dw", tag="yw3", align_bytes=64)
-    dealt_scales = pool.tile([P, H], U8, name=name + "_ds", tag="yw2", align_bytes=64)
+    dealt_scales = pool.tile([P, H], U8, name=name + "_ds", tag="ht2", align_bytes=64)
     nc.vector.tensor_copy(
         dealt_words[:].rearrange("p (t m b) -> p m t b", t=PACK, b=2),
         words[:].rearrange("p (m t b) -> p m t b", t=PACK, b=2),
@@ -75,13 +77,13 @@ def tile_picked_coupled_none_po_kernel(
         w1dw = sb.tile([P, 2 * H], U8, name="w1dw", align_bytes=64)
         w1ds = sb.tile([P, H], U8, name="w1ds", align_bytes=64)
         w1s = sb.tile([P, H], U8, name="w1s", tag="raw_scales", align_bytes=64)
+        nc.gpsimd.memset(w1s[:].bitcast(I32), 0)
         nc.vector.memset(xs[:].bitcast(I32), 0)
-        nc.vector.memset(w1ds[:].bitcast(I32), 0)
         nc.sync.dma_start(offs_t[:], offs)
-        nc.scalar.dma_start(ww[:].bitcast(I32), w1_words[0].bitcast(I32))
-        load_scales([nc.sync, nc.scalar, nc.sync, nc.scalar], xs_rows, x_scales[0])
+        load_scales([nc.sync] * 4, xs_rows, x_scales[0])
+        nc.sync.dma_start(ww[:].bitcast(I32), w1_words[0].bitcast(I32))
         nc.sync.dma_start(xw[:].bitcast(I32), x_words[0].rearrange("p n t -> p (n t)").bitcast(I32))
-        load_scales([nc.scalar, nc.scalar, nc.scalar, nc.scalar], w1s, w1_scales[0])
+        load_scales([nc.sync, nc.sync, nc.sync, nc.sync], w1s, w1_scales[0])
         nc.sync.dma_start(p_t[0][:], p1)
         nc.sync.dma_start(p_t[1][:], p2)
         nc.sync.dma_start(q_t[0][:], q1)
@@ -100,8 +102,7 @@ def tile_picked_coupled_none_po_kernel(
             rows = slice(32 * q, 32 * q + 4)
             nc.vector.tensor_copy(xs[rows, :].bitcast(I32), xs_rows[rows, :].bitcast(I32))
         deal_runs(w1dw[:], ww[:])
-        for q in range(4):
-            deal_runs(w1ds[32 * q : 32 * q + 4, :], w1s[32 * q : 32 * q + 4, :])
+        deal_runs(w1ds[:], w1s[:])
         xgs = sb.tile([P, S], U8, name="xgs", align_bytes=64)
         nc.vector.tensor_copy(xgs[:], xs[:].indirect(offs_t[:]))
         xg = sb.tile([P, S], U32, name="xg", align_bytes=64)
@@ -126,8 +127,11 @@ def tile_picked_coupled_none_po_kernel(
         def new_bank(n, name):
             return ps.tile([P, 512], F32, name=name, tag=f"bank{n}")
 
-        yw = [sb.tile([P, S], F32, name=f"yw{t}", tag=f"yw{t}", align_bytes=64) for t in range(PACK)]
-        yp = [sb.tile([P, S], F32, name=f"yp{t}") for t in range(PACK)]
+        yw = [sb.tile([P, 2 * S], F32, name=f"yw{t}", tag=f"yw{t}", align_bytes=64) for t in range(PACK)]
+        hw = [sb.tile([P, 2 * S], F32, name=f"hw{t}") for t in range(PACK)]
+        yp = [hw[t][:, S:] for t in range(PACK)]
+        for t in range(PACK):
+            nc.gpsimd.memset(yw[t][:, S:], 0.0)
         for a in range(2):
             cols = slice(HALF * a, HALF * (a + 1))
             bank = new_bank(a, f"y0_{a}")[:, :HALF]
@@ -142,72 +146,112 @@ def tile_picked_coupled_none_po_kernel(
             y_banks[t] = new_bank(1 + t, f"y{t}")
             product(y_banks[t][:], w1dw, w1ds, t, xg[:], xgs[:])
 
-        ws = sb.tile([P, H], U8, name="ws", tag="raw_scales", align_bytes=64)
-        nc.gpsimd.memset(ws[:].bitcast(I32), 0)
+        ws = w1s
         nc.sync.dma_start(ww[:].bitcast(I32), w2_words[0].bitcast(I32))
         load_scales([nc.sync] * 4, ws, w2_scales[0])
         gain_rows = sb.tile([P, H], F32, name="gain_rows", tag="early", align_bytes=64)
         nc.sync.dma_start(gain_rows[:], gn.rearrange("f o -> (f o)").partition_broadcast(P))
 
-        def pulls(window, plain, pair, c0, w, name):
-            d = sb.tile([P, 2, w], F32, name="d" + name, tag="d", bufs=3)
-            for i in range(2):
-                nc.vector.tensor_tensor(
-                    d[:, i, :], window[:].indirect(pair[i][:, c0 // 16 : (c0 + w) // 16]), plain[:, c0 : c0 + w], SUB
-                )
-            pull = sb.tile([P, 2, w], F32, name="pull" + name, tag="pull", bufs=4)
-            nc.scalar.activation(pull[:], d[:], TANH, scale=0.5)
+        def difference(window, plain, offsets, c0, w, name):
+            d = sb.tile([P, w], F32, name=f"d{name}", tag="d", bufs=6)
+            nc.vector.tensor_tensor(
+                d[:], window[:].indirect(offsets[:, c0 // 16 : (c0 + w) // 16]), plain[:, c0 : c0 + w], SUB
+            )
+            return d
+
+        def pull_of(src, w, name):
+            pull = sb.tile([P, w], F32, name=f"pull{name}", tag="pull", bufs=6)
+            nc.scalar.activation(pull[:], src, TANH, scale=0.5)
             return pull
 
-        hw = [sb.tile([P, S], F32, name=f"hw{t}") for t in range(PACK)]
+        def pulls(window, plain, pair, c0, w, name):
+            return [pull_of(difference(window, plain, pair[i], c0, w, f"{name}_{i}")[:], w, f"{name}_{i}") for i in range(2)]
+
         hp = [sb.tile([P, S], F32, name=f"hp{t}") for t in range(PACK)]
-        ht = [sb.tile([P, S], F32, name=f"ht{t}") for t in range(PACK)]
+        ht = [sb.tile([P, S], F32, name=f"ht{t}", tag=f"ht{t}", align_bytes=64) for t in range(PACK)]
         ht_banks = {}
         zt_banks = {}
+        kept = {}
 
         def y_window(t):
-            nc.scalar.activation(yw[t][:], y_banks[t][:], COPY, scale=2.0)
-            if t > 1:
-                nc.sync.dma_start(yp[t][:], yw[t][:])
+            nc.scalar.activation(yw[t][:, :S], y_banks[t][:], COPY, scale=2.0)
+            if "SSDD"[t] == "D":
+                nc.sync.dma_start(yp[t], yw[t][:, :S])
 
-        def step1(t, a):
-            if a == 0:
+        def y_plain(t):
+            if "SSDD"[t] == "S":
+                nc.scalar.activation(yp[t], y_banks[t][:], COPY, scale=2.0)
+            if "SSDD"[t] == "V":
+                nc.vector.tensor_scalar(yp[t], y_banks[t][:], 2.0, None, MULT)
+
+        def step1(t, c0, w):
+            mode = "TTTT"[t]
+            if mode == "B":
+                kept[t] = []
+                for i in range(2):
+                    d = difference(yw[t], yp[t], p_t[i], c0, w, f"1_{t}_{c0}_{i}")
+                    bank = new_bank(5 + i, f"dt_bank{t}_{i}")
+                    for j0 in range(0, S, BLK):
+                        turned_sum(bank[:, j0 : j0 + BLK], [d[:, j0 : j0 + BLK]])
+                    kept[t].append(pull_of(bank[:], w, f"1_{t}_{c0}_{i}"))
+                return
+            pull = pulls(yw[t], yp[t], p_t, c0, w, f"1_{t}_{c0}")
+            if mode == "V":
+                kept[t] = pull
+                return
+            if c0 == 0:
                 ht_banks[t] = new_bank(5 + t % 2, f"ht_bank{t}")
-            pull = pulls(yw[t], yp[t], p_t, HALF * a, HALF, f"1_{t}_{a}")
-            for b0 in range(0, HALF, BLK):
-                blk = slice(HALF * a + b0, HALF * a + b0 + BLK)
-                sub = slice(b0, b0 + BLK)
-                turned_sum(ht_banks[t][:, blk], [yp[t][:, blk], pull[:, 0, sub], pull[:, 1, sub]])
+            for j0 in range(c0, c0 + w, BLK):
+                blk = slice(j0, j0 + BLK)
+                sub = slice(j0 - c0, j0 - c0 + BLK)
+                turned_sum(ht_banks[t][:, blk], [yp[t][:, blk], pull[0][:, sub], pull[1][:, sub]])
 
         def h_turned(t):
-            nc.scalar.copy(ht[t][:], ht_banks[t][:])
+            if "TTTT"[t] == "T":
+                nc.scalar.copy(ht[t][:], ht_banks[t][:])
+            if "TTTT"[t] == "V":
+                nc.vector.tensor_tensor(ht[t][:], kept[t][0][:], yp[t], ADD)
 
         def h_window(t):
-            bank = new_bank(0 if t % 2 else 7, f"h_bank{t}")
-            for j0 in range(0, S, BLK):
-                turned_sum(bank[:, j0 : j0 + BLK], [ht[t][:, j0 : j0 + BLK]])
-            nc.scalar.copy(hw[t][:], bank[:])
-            if t >= 3:
-                nc.scalar.copy(hp[t][:], bank[:])
+            mode = "TTTT"[t]
+            src = hw[t][:, :S]
+            if mode == "V":
+                nc.vector.tensor_tensor(hw[t][:, :S], kept[t][1][:], ht[t][:], ADD)
             else:
-                nc.sync.dma_start(hp[t][:], hw[t][:])
+                bank = new_bank(0 if t % 2 else 7, f"h_bank{t}")
+                for j0 in range(0, S, BLK):
+                    terms = [ht[t]] if mode == "T" else kept[t]
+                    turned_sum(bank[:, j0 : j0 + BLK], [x[:, j0 : j0 + BLK] for x in terms])
+                if mode == "T":
+                    nc.scalar.copy(hw[t][:, :S], bank[:])
+                    src = bank[:]
+                else:
+                    nc.vector.tensor_tensor(hw[t][:, :S], bank[:], yp[t], ADD)
+            if "VVSS"[t] == "S":
+                nc.scalar.copy(hp[t][:], src)
+            elif "VVSS"[t] == "V":
+                nc.vector.tensor_copy(hp[t][:], hw[t][:, :S])
+            else:
+                nc.sync.dma_start(hp[t][:], hw[t][:, :S])
 
         def step2(c, t):
             c0, w = CHUNKS[c]
-            pull = pulls(hw[t], hp[t], q_t, c0, w, f"2_{c}_{t}")
+            window, plain = (hw[t], hp[t]) if c == 0 else (hp[t], hw[t])
+            pull = pulls(window, plain, q_t, c0, w, f"2_{c}_{t}")
             for j0 in range(c0, c0 + w, BLK):
                 if t == 0:
                     zt_banks[j0] = new_bank(1 + j0 // BLK, f"zt_bank{j0}")
                 sub = slice(j0 - c0, j0 - c0 + BLK)
                 turned_sum(
                     zt_banks[j0][:].rearrange("j (g t r) -> j t g r", t=PACK, g=8)[:, t],
-                    [hp[t][:, j0 : j0 + BLK], pull[:, 0, sub], pull[:, 1, sub]],
+                    [hp[t][:, j0 : j0 + BLK], pull[0][:, sub], pull[1][:, sub]],
                 )
 
         ow = sb.tile([P, S], U32, name="ow", align_bytes=64)
         osc = sb.tile([P, S], U8, name="osc", align_bytes=64)
         out_rows = out_0.rearrange("(p t) j -> p t j", t=PACK)
         out_words = out_1[0].rearrange("p n t -> p (n t)").bitcast(I32)
+        ofs = [sb.tile([P, PACK, HALF], F32, name=f"of{a}") for a in range(2)]
         zts = {j0: sb.tile([P, H], BF16, name=f"zt{j0}") for j0 in range(0, S, BLK)}
 
         def scale_z(j0, pick):
@@ -215,10 +259,11 @@ def tile_picked_coupled_none_po_kernel(
 
         def finish(j0):
             n = j0 // BLK
-            last = j0 + BLK == S
             blk = slice(j0, j0 + BLK)
             zt = zts[j0]
-            bank = new_bank(5 + n % 2, f"z_bank{j0}")
+            of = ofs[j0 // HALF]
+            part = slice(j0 % HALF, j0 % HALF + BLK)
+            bank = new_bank((5 + n) % 8, f"z_bank{j0}")
             words = zt[:].bitcast(F32).rearrange("j (p u) -> j u p", u=2)
             for u in range(2):
                 turned_sum(bank[:, BLK * u : BLK * (u + 1)], [words[:, u, :]])
@@ -230,50 +275,50 @@ def tile_picked_coupled_none_po_kernel(
             zc = sb.tile([P, BLK], U32, name=f"zc{j0}", align_bytes=64)
             zs = sb.tile([P, BLK], U8, name=f"zs{j0}", align_bytes=64)
             nc.vector.quantize_mx(out=zc[:].bitcast(FP8X4), scales=zs[:], in_=zi[:])
-            bank = new_bank(0 if n % 2 else 7, f"o_bank{j0}")
+            bank = new_bank(1 + n, f"o_bank{j0}")
             for t in range(PACK):
                 product(bank[:, BLK * t : BLK * (t + 1)], w2dw, w2ds, t, zc[:], zs[:])
             oi = sb.tile([P, PACK * BLK], BF16, name=f"oi{j0}", align_bytes=64)
-            copy = nc.vector.tensor_copy if last else nc.scalar.copy
-            copy(oi[:].rearrange("p (j t) -> p j t", t=PACK), bank[:].rearrange("p (t j) -> p j t", t=PACK))
-            of = sb.tile([P, PACK, BLK], F32, name=f"of{j0}")
-            nc.scalar.copy(of[:], bank[:].rearrange("p (t j) -> p t j", t=PACK))
+            if "BBBB"[n] == "B":
+                nc.scalar.copy(of[:, :, part], bank[:].rearrange("p (t j) -> p t j", t=PACK))
+                interleave(nc.vector.tensor_copy, oi[:], of[:, :, part])
+            else:
+                copy = nc.vector.tensor_copy if "BBBB"[n] == "V" else nc.scalar.copy
+                copy(oi[:].rearrange("p (j t) -> p j t", t=PACK), bank[:].rearrange("p (t j) -> p j t", t=PACK))
+                nc.scalar.copy(of[:, :, part], bank[:].rearrange("p (t j) -> p t j", t=PACK))
             nc.vector.quantize_mx(out=ow[:, blk].bitcast(FP8X4), scales=osc[:, blk], in_=oi[:])
-            nc.sync.dma_start(out_rows[:, :, blk], of[:])
-            nc.sync.dma_start(out_words[:, blk], ow[:, blk].bitcast(I32))
+            if n in ROW_STORES:
+                cols = slice(ROW_STORES[n], j0 + BLK)
+                nc.sync.dma_start(out_rows[:, :, cols], of[:])
+            if n in WORD_STORES:
+                cols = slice(WORD_STORES[n], j0 + BLK)
+                nc.sync.dma_start(out_words[:, cols], ow[:, cols].bitcast(I32))
 
         y_window(1)
-        step1(0, 0)
-        nc.scalar.activation(yp[1][:], y_banks[1][:], COPY, scale=2.0)
-        step1(0, 1)
         y_window(2)
+        y_plain(1)
+        step1(0, 0, HALF)
+        y_window(3)
+        step1(0, HALF, HALF)
+        y_plain(2)
+        y_plain(3)
         for t in range(1, PACK):
-            step1(t, 0)
+            step1(t, 0, S)
             h_turned(t - 1)
-            if t == 1:
-                y_window(3)
-            step1(t, 1)
             h_window(t - 1)
-        step2(0, 0)
         h_turned(3)
-        step2(0, 1)
         h_window(3)
-        step2(1, 0)
-        step2(1, 1)
         w2dw, w2ds = deal_columns(nc, sb, "w2", ww, ws)
-        step2(0, 2)
-        step2(0, 3)
-        for j0 in (0, BLK):
+        for t in range(PACK):
+            step2(0, t)
+        for t in range(PACK):
+            step2(1, t)
+            if t == 9:
+                scale_z(0, lambda ap: ap)
+                finish(0)
+        for j0 in range(0, S, BLK):
             scale_z(j0, lambda ap: ap)
             finish(j0)
-        step2(1, 2)
-        step2(1, 3)
-        scale_z(2 * BLK, lambda ap: ap)
-        finish(2 * BLK)
-        for t in range(PACK):
-            step2(2, t)
-        scale_z(3 * BLK, lambda ap: ap)
-        finish(3 * BLK)
         for q in range(4):
             queue = nc.scalar if q % 2 else nc.sync
             queue.dma_start(out_2[0][4 * q : 4 * q + 4, :].bitcast(I32), osc[32 * q : 32 * q + 4, :].bitcast(I32))

@@ -14,7 +14,6 @@ U16 = mybir.dt.uint16
 U8 = mybir.dt.uint8
 FP8X4 = mybir.dt.float8_e4m3fn_x4
 FP4X4 = mybir.dt.float4_e2m1fn_x4
-ADD = mybir.AluOpType.add
 SUB = mybir.AluOpType.subtract
 MULT = mybir.AluOpType.mult
 COPY = mybir.ActivationFunctionType.Copy
@@ -22,37 +21,25 @@ TANH = mybir.ActivationFunctionType.Tanh
 
 P = 128
 PACK = 4
-HALF = 256
+TILES = 4
+GROUPS = 8
+QUADS = 4
+PER_COLUMN = 16
+HALF = S // 2
 BLK = 128
-ROW_STORES = {1: 0, 3: 256}
-WORD_STORES = {2: 0, 3: 384}
-CHUNKS = ((0, 384), (384, 128))
+BANK = 512
+RING = 6
+LONG = S - BLK
+LATE = 2
 
 
-def load_scales(queues, tile, rows):
-    for q in range(4):
-        queues[q].dma_start(tile[32 * q : 32 * q + 4, :].bitcast(I32), rows[4 * q : 4 * q + 4, :].bitcast(I32))
+def load_scales(nc, tile, rows):
+    for q in range(QUADS):
+        nc.sync.dma_start(tile[32 * q : 32 * q + 4, :].bitcast(I32), rows[4 * q : 4 * q + 4, :].bitcast(I32))
 
 
-def deal_columns(nc, pool, name, words, scales):
-    dealt_words = pool.tile([P, 2 * H], U8, name=name + "_dw", tag="yw3", align_bytes=64)
-    dealt_scales = pool.tile([P, H], U8, name=name + "_ds", tag="ht2", align_bytes=64)
-    nc.vector.tensor_copy(
-        dealt_words[:].rearrange("p (t m b) -> p m t b", t=PACK, b=2),
-        words[:].rearrange("p (m t b) -> p m t b", t=PACK, b=2),
-    )
-    nc.vector.tensor_copy(
-        dealt_scales[:].rearrange("p (t m) -> p m t", t=PACK),
-        scales[:].rearrange("p (m t) -> p m t", t=PACK),
-    )
-    return dealt_words, dealt_scales
-
-
-def interleave(engine_copy, dst, src):
-    engine_copy(
-        dst.rearrange("p (c i t) -> p c t i", i=4, t=PACK),
-        src.rearrange("p t (c i) -> p c t i", i=4),
-    )
+def entries(offsets, first, count):
+    return offsets[:, first // PER_COLUMN : (first + count) // PER_COLUMN]
 
 
 def tile_picked_coupled_none_po_kernel(
@@ -64,56 +51,49 @@ def tile_picked_coupled_none_po_kernel(
         sb = ctx.enter_context(tc.tile_pool(name="sb", bufs=1))
         ps = ctx.enter_context(tc.psum_pool(name="ps", bufs=1))
 
-        offs_t = lists.tile([P, S // 16], U16, name="offs_t")
-        p_t = [lists.tile([P, S // 16], U16, name=f"p_t{i}") for i in range(2)]
-        q_t = [lists.tile([P, S // 16], U16, name=f"q_t{i}") for i in range(2)]
+        picks = lists.tile([P, S // PER_COLUMN], U16, name="picks")
+        p_lists = [lists.tile([P, S // PER_COLUMN], U16, name=f"p_list{i}") for i in range(2)]
+        q_lists = [lists.tile([P, S // PER_COLUMN], U16, name=f"q_list{i}") for i in range(2)]
 
-        xw = sb.tile([P, T], U32, name="xw", align_bytes=64)
-        xs_rows = sb.tile([P, T], U8, name="xs_rows", tag="early", align_bytes=64)
-        xs = sb.tile([P, T], U8, name="xs", align_bytes=64)
-        ww = sb.tile([P, 2 * H], U8, name="ww", align_bytes=64)
+        x_table = sb.tile([P, T], U32, name="x_table", align_bytes=64)
+        x_rows = sb.tile([P, T], U8, name="x_rows", tag="rows_then_gain", align_bytes=64)
+        x_plane = sb.tile([P, T], U8, name="x_plane", align_bytes=64)
+        raw_words = sb.tile([P, 2 * H], U8, name="raw_words", align_bytes=64)
         ident = sb.tile([P, P], F32, name="ident")
-
-        w1dw = sb.tile([P, 2 * H], U8, name="w1dw", align_bytes=64)
-        w1ds = sb.tile([P, H], U8, name="w1ds", align_bytes=64)
-        w1s = sb.tile([P, H], U8, name="w1s", tag="raw_scales", align_bytes=64)
-        nc.gpsimd.memset(w1s[:].bitcast(I32), 0)
-        nc.vector.memset(xs[:].bitcast(I32), 0)
-        nc.sync.dma_start(offs_t[:], offs)
-        load_scales([nc.sync] * 4, xs_rows, x_scales[0])
-        nc.sync.dma_start(ww[:].bitcast(I32), w1_words[0].bitcast(I32))
-        nc.sync.dma_start(xw[:].bitcast(I32), x_words[0].rearrange("p n t -> p (n t)").bitcast(I32))
-        load_scales([nc.sync, nc.sync, nc.sync, nc.sync], w1s, w1_scales[0])
-        nc.sync.dma_start(p_t[0][:], p1)
-        nc.sync.dma_start(p_t[1][:], p2)
-        nc.sync.dma_start(q_t[0][:], q1)
-        nc.sync.dma_start(q_t[1][:], q2)
+        w1_dealt = sb.tile([P, 2 * H], U8, name="w1_dealt", align_bytes=64)
+        w1_plane = sb.tile([P, H], U8, name="w1_plane", align_bytes=64)
+        raw_plane = sb.tile([P, H], U8, name="raw_plane", align_bytes=64)
+        nc.gpsimd.memset(raw_plane[:].bitcast(I32), 0)
+        nc.vector.memset(x_plane[:].bitcast(I32), 0)
+        nc.sync.dma_start(picks[:], offs)
+        load_scales(nc, x_rows, x_scales[0])
+        nc.sync.dma_start(raw_words[:].bitcast(I32), w1_words[0].bitcast(I32))
+        nc.sync.dma_start(x_table[:].bitcast(I32), x_words[0].rearrange("p n s -> p (n s)").bitcast(I32))
+        load_scales(nc, raw_plane, w1_scales[0])
+        for tile, source in zip(p_lists + q_lists, (p1, p2, q1, q2)):
+            nc.sync.dma_start(tile[:], source)
         make_identity(nc, ident[:])
-        warm = sb.tile([P, 1], F32, name="warm")
-        nc.scalar.activation(warm[:], ident[:, 0:1], TANH)
 
-        def deal_runs(dealt, raw):
+        for q in range(QUADS):
+            rows = slice(32 * q, 32 * q + 4)
+            nc.vector.tensor_copy(x_plane[rows, :].bitcast(I32), x_rows[rows, :].bitcast(I32))
+        for dealt, raw in ((w1_dealt, raw_words), (w1_plane, raw_plane)):
             nc.vector.tensor_copy(
-                dealt.bitcast(I32).rearrange("p (t g x) -> p t g x", t=PACK, g=8),
-                raw.bitcast(I32).rearrange("p (g t x) -> p t g x", t=PACK, g=8),
+                dealt[:].bitcast(I32).rearrange("p (t g x) -> p t g x", t=TILES, g=GROUPS),
+                raw[:].bitcast(I32).rearrange("p (g t x) -> p t g x", t=TILES, g=GROUPS),
             )
 
-        for q in range(4):
-            rows = slice(32 * q, 32 * q + 4)
-            nc.vector.tensor_copy(xs[rows, :].bitcast(I32), xs_rows[rows, :].bitcast(I32))
-        deal_runs(w1dw[:], ww[:])
-        deal_runs(w1ds[:], w1s[:])
-        xgs = sb.tile([P, S], U8, name="xgs", align_bytes=64)
-        nc.vector.tensor_copy(xgs[:], xs[:].indirect(offs_t[:]))
-        xg = sb.tile([P, S], U32, name="xg", align_bytes=64)
-        for a in range(2):
-            nc.vector.tensor_copy(xg[:, HALF * a : HALF * (a + 1)], xw[:].indirect(offs_t[:, 16 * a : 16 * (a + 1)]))
+        picked_plane = sb.tile([P, S], U8, name="picked_plane", align_bytes=64)
+        nc.vector.tensor_copy(picked_plane[:], x_plane[:].indirect(picks[:]))
+        picked = sb.tile([P, S], U32, name="picked", align_bytes=64)
+        for first in (0, HALF):
+            nc.vector.tensor_copy(picked[:, first : first + HALF], x_table[:].indirect(entries(picks, first, HALF)))
 
-        def product(bank, dw, ds, t, codes, scales):
+        def product(out, dealt, plane, t, codes, scales):
             nc.tensor.matmul_mx(
-                out=bank,
-                lhsT=dw[:, 2 * P * t : 2 * P * (t + 1)].bitcast(FP4X4),
-                lhsT_scale=ds[:, P * t : P * (t + 1)],
+                out=out,
+                lhsT=dealt[:, 2 * P * t : 2 * P * (t + 1)].bitcast(FP4X4),
+                lhsT_scale=plane[:, P * t : P * (t + 1)],
                 rhs=codes.bitcast(FP8X4),
                 rhs_scale=scales,
                 start=True,
@@ -124,201 +104,158 @@ def tile_picked_coupled_none_po_kernel(
             for n, term in enumerate(terms):
                 nc.tensor.matmul(out, term, ident[:], start=n == 0, stop=n == len(terms) - 1, is_transpose=True)
 
-        def new_bank(n, name):
-            return ps.tile([P, 512], F32, name=name, tag=f"bank{n}")
+        def new_bank(number, name):
+            return ps.tile([P, BANK], F32, name=name, tag=f"bank{number}")
 
-        yw = [sb.tile([P, 2 * S], F32, name=f"yw{t}", tag=f"yw{t}", align_bytes=64) for t in range(PACK)]
-        hw = [sb.tile([P, 2 * S], F32, name=f"hw{t}") for t in range(PACK)]
-        yp = [hw[t][:, S:] for t in range(PACK)]
-        for t in range(PACK):
-            nc.gpsimd.memset(yw[t][:, S:], 0.0)
-        for a in range(2):
-            cols = slice(HALF * a, HALF * (a + 1))
-            bank = new_bank(a, f"y0_{a}")[:, :HALF]
-            product(bank, w1dw, w1ds, 0, xg[:, cols], xgs[:, cols])
-            nc.scalar.activation(yw[0][:, cols], bank, COPY, scale=2.0)
-            if a == 0:
-                nc.vector.tensor_scalar(yp[0][:, cols], bank, 2.0, None, MULT)
+        y_window = [sb.tile([P, 2 * S], F32, name=f"y_window{t}", tag=f"y_window{t}", align_bytes=64) for t in range(TILES)]
+        h_window = [sb.tile([P, 2 * S], F32, name=f"h_window{t}") for t in range(TILES)]
+        y_plain = [h_window[t][:, S:] for t in range(TILES)]
+        for t in range(TILES):
+            engine = nc.vector if t < TILES // 2 else nc.gpsimd
+            engine.memset(y_window[t][:, S:], 0.0)
+
+        for first in (0, HALF):
+            cols = slice(first, first + HALF)
+            bank = new_bank(first // HALF, f"y0_bank{first}")[:, :HALF]
+            product(bank, w1_dealt, w1_plane, 0, picked[:, cols], picked_plane[:, cols])
+            nc.scalar.activation(y_window[0][:, cols], bank, COPY, scale=2.0)
+            if first == 0:
+                nc.vector.tensor_scalar(y_plain[0][:, cols], bank, 2.0, None, MULT)
             else:
-                nc.scalar.activation(yp[0][:, cols], bank, COPY, scale=2.0)
+                nc.scalar.activation(y_plain[0][:, cols], bank, COPY, scale=2.0)
         y_banks = {}
-        for t in range(1, PACK):
-            y_banks[t] = new_bank(1 + t, f"y{t}")
-            product(y_banks[t][:], w1dw, w1ds, t, xg[:], xgs[:])
+        for t in range(1, TILES):
+            y_banks[t] = new_bank(1 + t, f"y{t}_bank")
+            product(y_banks[t][:], w1_dealt, w1_plane, t, picked[:], picked_plane[:])
 
-        ws = w1s
-        nc.sync.dma_start(ww[:].bitcast(I32), w2_words[0].bitcast(I32))
-        load_scales([nc.sync] * 4, ws, w2_scales[0])
-        gain_rows = sb.tile([P, H], F32, name="gain_rows", tag="early", align_bytes=64)
+        nc.sync.dma_start(raw_words[:].bitcast(I32), w2_words[0].bitcast(I32))
+        load_scales(nc, raw_plane, w2_scales[0])
+        gain_rows = sb.tile([P, H], F32, name="gain_rows", tag="rows_then_gain", align_bytes=64)
         nc.sync.dma_start(gain_rows[:], gn.rearrange("f o -> (f o)").partition_broadcast(P))
 
-        def difference(window, plain, offsets, c0, w, name):
-            d = sb.tile([P, w], F32, name=f"d{name}", tag="d", bufs=6)
-            nc.vector.tensor_tensor(
-                d[:], window[:].indirect(offsets[:, c0 // 16 : (c0 + w) // 16]), plain[:, c0 : c0 + w], SUB
-            )
-            return d
+        h_plain = [sb.tile([P, S], F32, name=f"h_plain{t}") for t in range(TILES)]
+        h_turned = [sb.tile([P, S], F32, name=f"h_turned{t}", tag=f"h_turned{t}", align_bytes=64) for t in range(TILES)]
+        h_sums = {}
+        z_sums = {}
 
-        def pull_of(src, w, name):
-            pull = sb.tile([P, w], F32, name=f"pull{name}", tag="pull", bufs=6)
-            nc.scalar.activation(pull[:], src, TANH, scale=0.5)
-            return pull
+        def pulls(window, plain, pair, first, count, name):
+            results = []
+            for i, offsets in enumerate(pair):
+                diff = sb.tile([P, count], F32, name=f"diff{name}_{i}", tag="diff", bufs=RING)
+                nc.vector.tensor_tensor(
+                    diff[:], window[:].indirect(entries(offsets, first, count)), plain[:, first : first + count], SUB
+                )
+                pull = sb.tile([P, count], F32, name=f"pull{name}_{i}", tag="pull", bufs=RING)
+                nc.scalar.activation(pull[:], diff[:], TANH, scale=0.5)
+                results.append(pull)
+            return results
 
-        def pulls(window, plain, pair, c0, w, name):
-            return [pull_of(difference(window, plain, pair[i], c0, w, f"{name}_{i}")[:], w, f"{name}_{i}") for i in range(2)]
+        def fill_y_window(t):
+            nc.scalar.activation(y_window[t][:, :S], y_banks[t][:], COPY, scale=2.0)
+            if t >= LATE:
+                nc.sync.dma_start(y_plain[t], y_window[t][:, :S])
 
-        hp = [sb.tile([P, S], F32, name=f"hp{t}") for t in range(PACK)]
-        ht = [sb.tile([P, S], F32, name=f"ht{t}", tag=f"ht{t}", align_bytes=64) for t in range(PACK)]
-        ht_banks = {}
-        zt_banks = {}
-        kept = {}
-
-        def y_window(t):
-            nc.scalar.activation(yw[t][:, :S], y_banks[t][:], COPY, scale=2.0)
-            if "SSDD"[t] == "D":
-                nc.sync.dma_start(yp[t], yw[t][:, :S])
-
-        def y_plain(t):
-            if "SSDD"[t] == "S":
-                nc.scalar.activation(yp[t], y_banks[t][:], COPY, scale=2.0)
-            if "SSDD"[t] == "V":
-                nc.vector.tensor_scalar(yp[t], y_banks[t][:], 2.0, None, MULT)
-
-        def step1(t, c0, w):
-            mode = "TTTT"[t]
-            if mode == "B":
-                kept[t] = []
-                for i in range(2):
-                    d = difference(yw[t], yp[t], p_t[i], c0, w, f"1_{t}_{c0}_{i}")
-                    bank = new_bank(5 + i, f"dt_bank{t}_{i}")
-                    for j0 in range(0, S, BLK):
-                        turned_sum(bank[:, j0 : j0 + BLK], [d[:, j0 : j0 + BLK]])
-                    kept[t].append(pull_of(bank[:], w, f"1_{t}_{c0}_{i}"))
-                return
-            pull = pulls(yw[t], yp[t], p_t, c0, w, f"1_{t}_{c0}")
-            if mode == "V":
-                kept[t] = pull
-                return
-            if c0 == 0:
-                ht_banks[t] = new_bank(5 + t % 2, f"ht_bank{t}")
-            for j0 in range(c0, c0 + w, BLK):
+        def first_step(t, first, count):
+            pull = pulls(y_window[t], y_plain[t], p_lists, first, count, f"1_{t}_{first}")
+            if first == 0:
+                h_sums[t] = new_bank(5 + t % 2, f"h_sum{t}")
+            for j0 in range(first, first + count, BLK):
                 blk = slice(j0, j0 + BLK)
-                sub = slice(j0 - c0, j0 - c0 + BLK)
-                turned_sum(ht_banks[t][:, blk], [yp[t][:, blk], pull[0][:, sub], pull[1][:, sub]])
+                part = slice(j0 - first, j0 - first + BLK)
+                turned_sum(h_sums[t][:, blk], [y_plain[t][:, blk], pull[0][:, part], pull[1][:, part]])
 
-        def h_turned(t):
-            if "TTTT"[t] == "T":
-                nc.scalar.copy(ht[t][:], ht_banks[t][:])
-            if "TTTT"[t] == "V":
-                nc.vector.tensor_tensor(ht[t][:], kept[t][0][:], yp[t], ADD)
-
-        def h_window(t):
-            mode = "TTTT"[t]
-            src = hw[t][:, :S]
-            if mode == "V":
-                nc.vector.tensor_tensor(hw[t][:, :S], kept[t][1][:], ht[t][:], ADD)
+        def fill_h(t):
+            nc.scalar.copy(h_turned[t][:], h_sums[t][:])
+            bank = new_bank(0 if t % 2 else 7, f"h_bank{t}")
+            for j0 in range(0, S, BLK):
+                turned_sum(bank[:, j0 : j0 + BLK], [h_turned[t][:, j0 : j0 + BLK]])
+            nc.scalar.copy(h_window[t][:, :S], bank[:])
+            if t >= LATE:
+                nc.scalar.copy(h_plain[t][:], bank[:])
             else:
-                bank = new_bank(0 if t % 2 else 7, f"h_bank{t}")
-                for j0 in range(0, S, BLK):
-                    terms = [ht[t]] if mode == "T" else kept[t]
-                    turned_sum(bank[:, j0 : j0 + BLK], [x[:, j0 : j0 + BLK] for x in terms])
-                if mode == "T":
-                    nc.scalar.copy(hw[t][:, :S], bank[:])
-                    src = bank[:]
-                else:
-                    nc.vector.tensor_tensor(hw[t][:, :S], bank[:], yp[t], ADD)
-            if "VVSS"[t] == "S":
-                nc.scalar.copy(hp[t][:], src)
-            elif "VVSS"[t] == "V":
-                nc.vector.tensor_copy(hp[t][:], hw[t][:, :S])
-            else:
-                nc.sync.dma_start(hp[t][:], hw[t][:, :S])
+                nc.vector.tensor_copy(h_plain[t][:], h_window[t][:, :S])
 
-        def step2(c, t):
-            c0, w = CHUNKS[c]
-            window, plain = (hw[t], hp[t]) if c == 0 else (hp[t], hw[t])
-            pull = pulls(window, plain, q_t, c0, w, f"2_{c}_{t}")
-            for j0 in range(c0, c0 + w, BLK):
+        def second_step(t, first, count):
+            window, plain = (h_window[t], h_plain[t]) if count == LONG else (h_plain[t], h_window[t])
+            pull = pulls(window, plain, q_lists, first, count, f"2_{t}_{first}")
+            for j0 in range(first, first + count, BLK):
                 if t == 0:
-                    zt_banks[j0] = new_bank(1 + j0 // BLK, f"zt_bank{j0}")
-                sub = slice(j0 - c0, j0 - c0 + BLK)
+                    z_sums[j0] = new_bank(1 + j0 // BLK, f"z_sum{j0}")
+                part = slice(j0 - first, j0 - first + BLK)
                 turned_sum(
-                    zt_banks[j0][:].rearrange("j (g t r) -> j t g r", t=PACK, g=8)[:, t],
-                    [hp[t][:, j0 : j0 + BLK], pull[0][:, sub], pull[1][:, sub]],
+                    z_sums[j0][:].rearrange("j (g t r) -> j t g r", t=TILES, g=GROUPS)[:, t],
+                    [h_plain[t][:, j0 : j0 + BLK], pull[0][:, part], pull[1][:, part]],
                 )
 
-        ow = sb.tile([P, S], U32, name="ow", align_bytes=64)
-        osc = sb.tile([P, S], U8, name="osc", align_bytes=64)
-        out_rows = out_0.rearrange("(p t) j -> p t j", t=PACK)
-        out_words = out_1[0].rearrange("p n t -> p (n t)").bitcast(I32)
-        ofs = [sb.tile([P, PACK, HALF], F32, name=f"of{a}") for a in range(2)]
-        zts = {j0: sb.tile([P, H], BF16, name=f"zt{j0}") for j0 in range(0, S, BLK)}
+        out_codes = sb.tile([P, S], U32, name="out_codes", align_bytes=64)
+        out_plane = sb.tile([P, S], U8, name="out_plane", align_bytes=64)
+        out_rows = out_0.rearrange("(p s) j -> p s j", s=PACK)
+        out_words = out_1[0].rearrange("p n s -> p (n s)").bitcast(I32)
+        out_halves = [sb.tile([P, PACK, HALF], F32, name=f"out_half{a}") for a in range(2)]
+        z_turned = {j0: sb.tile([P, H], BF16, name=f"z_turned{j0}") for j0 in range(0, S, BLK)}
 
-        def scale_z(j0, pick):
-            nc.vector.scalar_tensor_tensor(pick(zts[j0][:]), pick(zt_banks[j0][:]), 0.5, pick(gain_rows[:]), MULT, MULT)
-
-        def finish(j0):
-            n = j0 // BLK
+        def finish(j0, w2_dealt, w2_plane):
+            number = j0 // BLK
             blk = slice(j0, j0 + BLK)
-            zt = zts[j0]
-            of = ofs[j0 // HALF]
+            nc.vector.scalar_tensor_tensor(z_turned[j0][:], z_sums[j0][:], 0.5, gain_rows[:], MULT, MULT)
+            half = out_halves[j0 // HALF]
             part = slice(j0 % HALF, j0 % HALF + BLK)
-            bank = new_bank((5 + n) % 8, f"z_bank{j0}")
-            words = zt[:].bitcast(F32).rearrange("j (p u) -> j u p", u=2)
+            bank = new_bank((5 + number) % 8, f"z_bank{j0}")
+            pairs = z_turned[j0][:].bitcast(F32).rearrange("j (p u) -> j u p", u=2)
             for u in range(2):
-                turned_sum(bank[:, BLK * u : BLK * (u + 1)], [words[:, u, :]])
-            zi = sb.tile([P, PACK * BLK], BF16, name=f"zi{j0}", align_bytes=64)
+                turned_sum(bank[:, BLK * u : BLK * (u + 1)], [pairs[:, u, :]])
+            z_woven = sb.tile([P, PACK * BLK], BF16, name=f"z_woven{j0}", align_bytes=64)
             nc.scalar.copy(
-                zi[:].bitcast(F32).rearrange("p (j u) -> p j u", u=2),
+                z_woven[:].bitcast(F32).rearrange("p (j u) -> p j u", u=2),
                 bank[:, : 2 * BLK].rearrange("p (u j) -> p j u", u=2),
             )
-            zc = sb.tile([P, BLK], U32, name=f"zc{j0}", align_bytes=64)
-            zs = sb.tile([P, BLK], U8, name=f"zs{j0}", align_bytes=64)
-            nc.vector.quantize_mx(out=zc[:].bitcast(FP8X4), scales=zs[:], in_=zi[:])
-            bank = new_bank(1 + n, f"o_bank{j0}")
-            for t in range(PACK):
-                product(bank[:, BLK * t : BLK * (t + 1)], w2dw, w2ds, t, zc[:], zs[:])
-            oi = sb.tile([P, PACK * BLK], BF16, name=f"oi{j0}", align_bytes=64)
-            if "BBBB"[n] == "B":
-                nc.scalar.copy(of[:, :, part], bank[:].rearrange("p (t j) -> p t j", t=PACK))
-                interleave(nc.vector.tensor_copy, oi[:], of[:, :, part])
-            else:
-                copy = nc.vector.tensor_copy if "BBBB"[n] == "V" else nc.scalar.copy
-                copy(oi[:].rearrange("p (j t) -> p j t", t=PACK), bank[:].rearrange("p (t j) -> p j t", t=PACK))
-                nc.scalar.copy(of[:, :, part], bank[:].rearrange("p (t j) -> p t j", t=PACK))
-            nc.vector.quantize_mx(out=ow[:, blk].bitcast(FP8X4), scales=osc[:, blk], in_=oi[:])
-            if n in ROW_STORES:
-                cols = slice(ROW_STORES[n], j0 + BLK)
-                nc.sync.dma_start(out_rows[:, :, cols], of[:])
-            if n in WORD_STORES:
-                cols = slice(WORD_STORES[n], j0 + BLK)
-                nc.sync.dma_start(out_words[:, cols], ow[:, cols].bitcast(I32))
+            z_codes = sb.tile([P, BLK], U32, name=f"z_codes{j0}", align_bytes=64)
+            z_plane = sb.tile([P, BLK], U8, name=f"z_plane{j0}", align_bytes=64)
+            nc.vector.quantize_mx(out=z_codes[:].bitcast(FP8X4), scales=z_plane[:], in_=z_woven[:])
+            bank = new_bank(1 + number, f"out_bank{j0}")
+            for s in range(PACK):
+                product(bank[:, BLK * s : BLK * (s + 1)], w2_dealt, w2_plane, s, z_codes[:], z_plane[:])
+            out_woven = sb.tile([P, PACK * BLK], BF16, name=f"out_woven{j0}", align_bytes=64)
+            nc.scalar.copy(half[:, :, part], bank[:].rearrange("p (s j) -> p s j", s=PACK))
+            nc.vector.tensor_copy(
+                out_woven[:].rearrange("p (c i s) -> p c s i", i=4, s=PACK),
+                half[:, :, part].rearrange("p s (c i) -> p c s i", i=4),
+            )
+            nc.vector.quantize_mx(out=out_codes[:, blk].bitcast(FP8X4), scales=out_plane[:, blk], in_=out_woven[:])
+            end = j0 + BLK
+            if end % HALF == 0:
+                nc.sync.dma_start(out_rows[:, :, end - HALF : end], half[:])
+            if end in (LONG, S):
+                cols = slice(0 if end == LONG else LONG, end)
+                nc.sync.dma_start(out_words[:, cols], out_codes[:, cols].bitcast(I32))
 
-        y_window(1)
-        y_window(2)
-        y_plain(1)
-        step1(0, 0, HALF)
-        y_window(3)
-        step1(0, HALF, HALF)
-        y_plain(2)
-        y_plain(3)
-        for t in range(1, PACK):
-            step1(t, 0, S)
-            h_turned(t - 1)
-            h_window(t - 1)
-        h_turned(3)
-        h_window(3)
-        w2dw, w2ds = deal_columns(nc, sb, "w2", ww, ws)
-        for t in range(PACK):
-            step2(0, t)
-        for t in range(PACK):
-            step2(1, t)
-            if t == 9:
-                scale_z(0, lambda ap: ap)
-                finish(0)
+        fill_y_window(1)
+        fill_y_window(2)
+        nc.scalar.activation(y_plain[1], y_banks[1][:], COPY, scale=2.0)
+        first_step(0, 0, HALF)
+        fill_y_window(3)
+        first_step(0, HALF, HALF)
+        for t in range(1, TILES):
+            first_step(t, 0, S)
+            fill_h(t - 1)
+        fill_h(TILES - 1)
+
+        w2_dealt = sb.tile([P, 2 * N], U8, name="w2_dealt", tag=f"y_window{TILES - 1}", align_bytes=64)
+        w2_plane = sb.tile([P, N], U8, name="w2_plane", tag=f"h_turned{TILES - 2}", align_bytes=64)
+        nc.vector.tensor_copy(
+            w2_dealt[:].rearrange("p (s m b) -> p m s b", s=PACK, b=2),
+            raw_words[:].rearrange("p (m s b) -> p m s b", s=PACK, b=2),
+        )
+        nc.vector.tensor_copy(
+            w2_plane[:].rearrange("p (s m) -> p m s", s=PACK),
+            raw_plane[:].rearrange("p (m s) -> p m s", s=PACK),
+        )
+
+        for first, count in ((0, LONG), (LONG, S - LONG)):
+            for t in range(TILES):
+                second_step(t, first, count)
         for j0 in range(0, S, BLK):
-            scale_z(j0, lambda ap: ap)
-            finish(j0)
-        for q in range(4):
+            finish(j0, w2_dealt, w2_plane)
+        for q in range(QUADS):
             queue = nc.scalar if q % 2 else nc.sync
-            queue.dma_start(out_2[0][4 * q : 4 * q + 4, :].bitcast(I32), osc[32 * q : 32 * q + 4, :].bitcast(I32))
+            queue.dma_start(out_2[0][4 * q : 4 * q + 4, :].bitcast(I32), out_plane[32 * q : 32 * q + 4, :].bitcast(I32))

@@ -170,10 +170,7 @@ def tile_picked_coupled_none_po_kernel(
             for j0 in range(0, S, BLK):
                 turned_sum(bank[:, j0 : j0 + BLK], [h_turned[t][:, j0 : j0 + BLK]])
             nc.scalar.copy(h_window[t][:, :S], bank[:])
-            if t >= LATE:
-                nc.scalar.copy(h_plain[t][:], bank[:])
-            else:
-                nc.vector.tensor_copy(h_plain[t][:], h_window[t][:, :S])
+            nc.scalar.copy(h_plain[t][:], bank[:])
 
         def second_step(t, first, count):
             window, plain = (h_window[t], h_plain[t]) if count == LONG else (h_plain[t], h_window[t])

from contextlib import ExitStack

import concourse.mybir as mybir
from concourse.masks import make_identity

K, T, S, H, N = 512, 2048, 512, 512, 512
FLOPS = 2 * K * H * S + 2 * H * N * S

F32 = mybir.dt.float32
BF16 = mybir.dt.bfloat16
I32 = mybir.dt.int32
U32 = mybir.dt.uint32
U16 = mybir.dt.uint16
U8 = mybir.dt.uint8
FP8X4 = mybir.dt.float8_e4m3fn_x4
FP4X4 = mybir.dt.float4_e2m1fn_x4
SUB = mybir.AluOpType.subtract
MULT = mybir.AluOpType.mult
COPY = mybir.ActivationFunctionType.Copy
TANH = mybir.ActivationFunctionType.Tanh

P = 128
PACK = 4
TILES = 4
GROUPS = 8
QUADS = 4
PER_COLUMN = 16
HALF = S // 2
BLK = 128
BANK = 512
RING = 6
LONG = S - BLK
LATE = 2


def load_scales(nc, tile, rows):
    for q in range(QUADS):
        nc.sync.dma_start(tile[32 * q : 32 * q + 4, :].bitcast(I32), rows[4 * q : 4 * q + 4, :].bitcast(I32))


def entries(offsets, first, count):
    return offsets[:, first // PER_COLUMN : (first + count) // PER_COLUMN]


def tile_picked_coupled_none_po_kernel(
    tc, x_words, x_scales, w1_words, w1_scales, gn, w2_words, w2_scales, offs, p1, p2, q1, q2, out_0, out_1, out_2
):
    nc = tc.nc
    with ExitStack() as ctx:
        lists = ctx.enter_context(tc.tile_pool(name="lists", bufs=1))
        sb = ctx.enter_context(tc.tile_pool(name="sb", bufs=1))
        ps = ctx.enter_context(tc.psum_pool(name="ps", bufs=1))

        picks = lists.tile([P, S // PER_COLUMN], U16, name="picks")
        p_lists = [lists.tile([P, S // PER_COLUMN], U16, name=f"p_list{i}") for i in range(2)]
        q_lists = [lists.tile([P, S // PER_COLUMN], U16, name=f"q_list{i}") for i in range(2)]

        x_table = sb.tile([P, T], U32, name="x_table", align_bytes=64)
        x_rows = sb.tile([P, T], U8, name="x_rows", tag="rows_then_gain", align_bytes=64)
        x_plane = sb.tile([P, T], U8, name="x_plane", align_bytes=64)
        raw_words = sb.tile([P, 2 * H], U8, name="raw_words", align_bytes=64)
        ident = sb.tile([P, P], F32, name="ident")
        w1_dealt = sb.tile([P, 2 * H], U8, name="w1_dealt", align_bytes=64)
        w1_plane = sb.tile([P, H], U8, name="w1_plane", align_bytes=64)
        raw_plane = sb.tile([P, H], U8, name="raw_plane", align_bytes=64)
        nc.gpsimd.memset(raw_plane[:].bitcast(I32), 0)
        nc.vector.memset(x_plane[:].bitcast(I32), 0)
        nc.sync.dma_start(picks[:], offs)
        load_scales(nc, x_rows, x_scales[0])
        nc.sync.dma_start(raw_words[:].bitcast(I32), w1_words[0].bitcast(I32))
        nc.sync.dma_start(x_table[:].bitcast(I32), x_words[0].rearrange("p n s -> p (n s)").bitcast(I32))
        load_scales(nc, raw_plane, w1_scales[0])
        for tile, source in zip(p_lists + q_lists, (p1, p2, q1, q2)):
            nc.sync.dma_start(tile[:], source)
        make_identity(nc, ident[:])

        for q in range(QUADS):
            rows = slice(32 * q, 32 * q + 4)
            nc.vector.tensor_copy(x_plane[rows, :].bitcast(I32), x_rows[rows, :].bitcast(I32))
        for dealt, raw in ((w1_dealt, raw_words), (w1_plane, raw_plane)):
            nc.vector.tensor_copy(
                dealt[:].bitcast(I32).rearrange("p (t g x) -> p t g x", t=TILES, g=GROUPS),
                raw[:].bitcast(I32).rearrange("p (g t x) -> p t g x", t=TILES, g=GROUPS),
            )

        picked_plane = sb.tile([P, S], U8, name="picked_plane", align_bytes=64)
        nc.vector.tensor_copy(picked_plane[:], x_plane[:].indirect(picks[:]))
        picked = sb.tile([P, S], U32, name="picked", align_bytes=64)
        for first in (0, HALF):
            nc.vector.tensor_copy(picked[:, first : first + HALF], x_table[:].indirect(entries(picks, first, HALF)))

        def product(out, dealt, plane, t, codes, scales):
            nc.tensor.matmul_mx(
                out=out,
                lhsT=dealt[:, 2 * P * t : 2 * P * (t + 1)].bitcast(FP4X4),
                lhsT_scale=plane[:, P * t : P * (t + 1)],
                rhs=codes.bitcast(FP8X4),
                rhs_scale=scales,
                start=True,
                stop=True,
            )

        def turned_sum(out, terms):
            for n, term in enumerate(terms):
                nc.tensor.matmul(out, term, ident[:], start=n == 0, stop=n == len(terms) - 1, is_transpose=True)

        def new_bank(number, name):
            return ps.tile([P, BANK], F32, name=name, tag=f"bank{number}")

        y_window = [sb.tile([P, 2 * S], F32, name=f"y_window{t}", tag=f"y_window{t}", align_bytes=64) for t in range(TILES)]
        h_window = [sb.tile([P, 2 * S], F32, name=f"h_window{t}") for t in range(TILES)]
        y_plain = [h_window[t][:, S:] for t in range(TILES)]
        for t in range(TILES):
            engine = nc.vector if t < TILES // 2 else nc.gpsimd
            engine.memset(y_window[t][:, S:], 0.0)

        for first in (0, HALF):
            cols = slice(first, first + HALF)
            bank = new_bank(first // HALF, f"y0_bank{first}")[:, :HALF]
            product(bank, w1_dealt, w1_plane, 0, picked[:, cols], picked_plane[:, cols])
            nc.scalar.activation(y_window[0][:, cols], bank, COPY, scale=2.0)
            if first == 0:
                nc.vector.tensor_scalar(y_plain[0][:, cols], bank, 2.0, None, MULT)
            else:
                nc.scalar.activation(y_plain[0][:, cols], bank, COPY, scale=2.0)
        y_banks = {}
        for t in range(1, TILES):
            y_banks[t] = new_bank(1 + t, f"y{t}_bank")
            product(y_banks[t][:], w1_dealt, w1_plane, t, picked[:], picked_plane[:])

        nc.sync.dma_start(raw_words[:].bitcast(I32), w2_words[0].bitcast(I32))
        load_scales(nc, raw_plane, w2_scales[0])
        gain_rows = sb.tile([P, H], F32, name="gain_rows", tag="rows_then_gain", align_bytes=64)
        nc.sync.dma_start(gain_rows[:], gn.rearrange("f o -> (f o)").partition_broadcast(P))

        h_plain = [sb.tile([P, S], F32, name=f"h_plain{t}") for t in range(TILES)]
        h_turned = [sb.tile([P, S], F32, name=f"h_turned{t}", tag=f"h_turned{t}", align_bytes=64) for t in range(TILES)]
        h_sums = {}
        z_sums = {}

        def pulls(window, plain, pair, first, count, name):
            results = []
            for i, offsets in enumerate(pair):
                diff = sb.tile([P, count], F32, name=f"diff{name}_{i}", tag="diff", bufs=RING)
                nc.vector.tensor_tensor(
                    diff[:], window[:].indirect(entries(offsets, first, count)), plain[:, first : first + count], SUB
                )
                pull = sb.tile([P, count], F32, name=f"pull{name}_{i}", tag="pull", bufs=RING)
                nc.scalar.activation(pull[:], diff[:], TANH, scale=0.5)
                results.append(pull)
            return results

        def fill_y_window(t):
            nc.scalar.activation(y_window[t][:, :S], y_banks[t][:], COPY, scale=2.0)
            if t >= LATE:
                nc.sync.dma_start(y_plain[t], y_window[t][:, :S])

        def first_step(t, first, count):
            pull = pulls(y_window[t], y_plain[t], p_lists, first, count, f"1_{t}_{first}")
            if first == 0:
                h_sums[t] = new_bank(5 + t % 2, f"h_sum{t}")
            for j0 in range(first, first + count, BLK):
                blk = slice(j0, j0 + BLK)
                part = slice(j0 - first, j0 - first + BLK)
                turned_sum(h_sums[t][:, blk], [y_plain[t][:, blk], pull[0][:, part], pull[1][:, part]])

        def fill_h(t):
            nc.scalar.copy(h_turned[t][:], h_sums[t][:])
            bank = new_bank(0 if t % 2 else 7, f"h_bank{t}")
            for j0 in range(0, S, BLK):
                turned_sum(bank[:, j0 : j0 + BLK], [h_turned[t][:, j0 : j0 + BLK]])
            nc.scalar.copy(h_window[t][:, :S], bank[:])
            nc.scalar.copy(h_plain[t][:], bank[:])

        def second_step(t, first, count):
            window, plain = (h_window[t], h_plain[t]) if count == LONG else (h_plain[t], h_window[t])
            pull = pulls(window, plain, q_lists, first, count, f"2_{t}_{first}")
            for j0 in range(first, first + count, BLK):
                if t == 0:
                    z_sums[j0] = new_bank(1 + j0 // BLK, f"z_sum{j0}")
                part = slice(j0 - first, j0 - first + BLK)
                turned_sum(
                    z_sums[j0][:].rearrange("j (g t r) -> j t g r", t=TILES, g=GROUPS)[:, t],
                    [h_plain[t][:, j0 : j0 + BLK], pull[0][:, part], pull[1][:, part]],
                )

        out_codes = sb.tile([P, S], U32, name="out_codes", align_bytes=64)
        out_plane = sb.tile([P, S], U8, name="out_plane", align_bytes=64)
        out_rows = out_0.rearrange("(p s) j -> p s j", s=PACK)
        out_words = out_1[0].rearrange("p n s -> p (n s)").bitcast(I32)
        out_halves = [sb.tile([P, PACK, HALF], F32, name=f"out_half{a}") for a in range(2)]
        z_turned = {j0: sb.tile([P, H], BF16, name=f"z_turned{j0}") for j0 in range(0, S, BLK)}

        def finish(j0, w2_dealt, w2_plane):
            number = j0 // BLK
            blk = slice(j0, j0 + BLK)
            nc.vector.scalar_tensor_tensor(z_turned[j0][:], z_sums[j0][:], 0.5, gain_rows[:], MULT, MULT)
            half = out_halves[j0 // HALF]
            part = slice(j0 % HALF, j0 % HALF + BLK)
            bank = new_bank((5 + number) % 8, f"z_bank{j0}")
            pairs = z_turned[j0][:].bitcast(F32).rearrange("j (p u) -> j u p", u=2)
            for u in range(2):
                turned_sum(bank[:, BLK * u : BLK * (u + 1)], [pairs[:, u, :]])
            z_woven = sb.tile([P, PACK * BLK], BF16, name=f"z_woven{j0}", align_bytes=64)
            nc.scalar.copy(
                z_woven[:].bitcast(F32).rearrange("p (j u) -> p j u", u=2),
                bank[:, : 2 * BLK].rearrange("p (u j) -> p j u", u=2),
            )
            z_codes = sb.tile([P, BLK], U32, name=f"z_codes{j0}", align_bytes=64)
            z_plane = sb.tile([P, BLK], U8, name=f"z_plane{j0}", align_bytes=64)
            nc.vector.quantize_mx(out=z_codes[:].bitcast(FP8X4), scales=z_plane[:], in_=z_woven[:])
            bank = new_bank(1 + number, f"out_bank{j0}")
            for s in range(PACK):
                product(bank[:, BLK * s : BLK * (s + 1)], w2_dealt, w2_plane, s, z_codes[:], z_plane[:])
            out_woven = sb.tile([P, PACK * BLK], BF16, name=f"out_woven{j0}", align_bytes=64)
            nc.scalar.copy(half[:, :, part], bank[:].rearrange("p (s j) -> p s j", s=PACK))
            nc.vector.tensor_copy(
                out_woven[:].rearrange("p (c i s) -> p c s i", i=4, s=PACK),
                half[:, :, part].rearrange("p s (c i) -> p c s i", i=4),
            )
            nc.vector.quantize_mx(out=out_codes[:, blk].bitcast(FP8X4), scales=out_plane[:, blk], in_=out_woven[:])
            end = j0 + BLK
            if end % HALF == 0:
                nc.sync.dma_start(out_rows[:, :, end - HALF : end], half[:])
            if end in (LONG, S):
                cols = slice(0 if end == LONG else LONG, end)
                nc.sync.dma_start(out_words[:, cols], out_codes[:, cols].bitcast(I32))

        fill_y_window(1)
        fill_y_window(2)
        nc.scalar.activation(y_plain[1], y_banks[1][:], COPY, scale=2.0)
        first_step(0, 0, HALF)
        fill_y_window(3)
        first_step(0, HALF, HALF)
        for t in range(1, TILES):
            first_step(t, 0, S)
            fill_h(t - 1)
        fill_h(TILES - 1)

        w2_dealt = sb.tile([P, 2 * N], U8, name="w2_dealt", tag=f"y_window{TILES - 1}", align_bytes=64)
        w2_plane = sb.tile([P, N], U8, name="w2_plane", tag=f"h_turned{TILES - 2}", align_bytes=64)
        nc.vector.tensor_copy(
            w2_dealt[:].rearrange("p (s m b) -> p m s b", s=PACK, b=2),
            raw_words[:].rearrange("p (m s b) -> p m s b", s=PACK, b=2),
        )
        nc.vector.tensor_copy(
            w2_plane[:].rearrange("p (s m) -> p m s", s=PACK),
            raw_plane[:].rearrange("p (m s) -> p m s", s=PACK),
        )

        for first, count in ((0, LONG), (LONG, S - LONG)):
            for t in range(TILES):
                second_step(t, first, count)
        for j0 in range(0, S, BLK):
            finish(j0, w2_dealt, w2_plane)
        for q in range(QUADS):
            queue = nc.scalar if q % 2 else nc.sync
            queue.dma_start(out_2[0][4 * q : 4 * q + 4, :].bitcast(I32), out_plane[32 * q : 32 * q + 4, :].bitcast(I32))
